import numpy as np
import ml_dtypes


def mxq(x, axis, fmt="e4m3"):
    dtype, down = {"e4m3": (ml_dtypes.float8_e4m3fn, 7), "e5m2": (ml_dtypes.float8_e5m2, 14)}[fmt]
    v = np.moveaxis(np.asarray(x, np.float32).astype(ml_dtypes.bfloat16).astype(np.float64), axis, -1)
    blocks = v.reshape(v.shape[:-1] + (-1, 32))
    amax = np.abs(blocks).max(-1, keepdims=True)
    byte = np.maximum(np.where(amax > 0, np.frexp(amax)[1] - 1 + 127, 0) - down, 1)
    scale = np.exp2(byte - 127.0)
    codes = (blocks / scale).astype(np.float32).astype(dtype).astype(np.float64)
    return np.moveaxis((codes * scale).reshape(v.shape), -1, axis)


WIDE = False


def mx_kscale(k):
    if not WIDE:
        return np.ones(k)
    levels = np.array([10, -10, 5, -5, 0])
    if k % 512:
        return np.exp2(np.random.permutation(np.resize(levels, k // 32))).repeat(32)
    a = np.empty((k // 512, 16))
    for p in range(k // 512):
        a[p, :8] = np.random.permutation(np.resize(levels, 8))
        for g in range(8):
            far = levels[np.abs(levels - a[p, g]) >= 10]
            a[p, g + 8] = far[np.random.randint(len(far))]
    return np.exp2(a.ravel()).repeat(32)


def f64(x):
    return np.asarray(x).astype(np.float64)


def striped(idx):
    return np.tile(np.asarray(idx).reshape(-1, 16).T, (8, 1)).astype(np.uint16)


def unstriped(offs):
    return offs[:16].T.reshape(-1).astype(np.int64)


E2M1 = np.array([0.0, 0.5, 1.0, 1.5, 2.0, 3.0, 4.0, 6.0, -0.0, -0.5, -1.0, -1.5, -2.0, -3.0, -4.0, -6.0])


def pack_weight(w, fmt):
    k, n = w.shape
    w = f64(np.asarray(w, np.float32).astype(ml_dtypes.bfloat16)).reshape(k // 32, 32, n)
    amax = np.abs(w).max(1)
    if fmt == "e4m3":
        byte = np.frexp(amax)[1] - 1 + 127 - 7
    else:
        mant, ex = np.frexp(amax / 6.0)
        byte = np.where(mant > 0.5, ex, ex - 1) + 127
    byte = np.clip(np.where(amax > 0, byte, 1), 1, 254)
    scaled = (w * np.exp2(127.0 - byte)[:, None, :]).reshape(k, n).astype(np.float32)
    by_word = np.ascontiguousarray(scaled.reshape(k // 512, 128, 4, n).transpose(0, 1, 3, 2))
    if fmt == "e4m3":
        words = by_word.astype(ml_dtypes.float8_e4m3fn).view(np.uint8)
    else:
        c = by_word.astype(ml_dtypes.float4_e2m1fn).view(np.uint8) & 0xF
        words = (c[..., 0::2] | (c[..., 1::2] << 4)).reshape(k // 512, 128, 2 * n)
    return np.ascontiguousarray(words), np.ascontiguousarray(byte.astype(np.uint8).reshape(k // 512, 16, n))


def unpack_weight(words, scales, fmt):
    g, _, n = scales.shape
    words = np.ascontiguousarray(words).reshape(g, 128, n, -1)
    if fmt == "e4m3":
        vals = words.view(ml_dtypes.float8_e4m3fn).astype(np.float64)
    else:
        nib = np.empty((g, 128, n, 4), np.uint8)
        nib[..., 0::2] = words & 0xF
        nib[..., 1::2] = words >> 4
        vals = E2M1[nib]
    vals = vals * np.repeat(np.exp2(scales.astype(np.float64) - 127.0), 8, axis=1)[..., None]
    return vals.transpose(0, 1, 3, 2).reshape(g * 512, n)


K, T, J, N = 1024, 1024, 512, 512


def setup_inputs():
    n = np.random.standard_normal
    idx = np.random.permutation(T)[:J]
    idx2 = np.random.permutation(T)[:J]
    idx3 = np.random.permutation(T)[:J]
    fk = mx_kscale(K)
    wp = pack_weight(n((K, N)) * 1 / np.sqrt(K) * fk[:, None], "e2m1")
    return {
        "xf": (n((K, T))).astype(np.float32),
        "fk": (np.random.uniform(0.5, 2.0, (K, 1)) / fk[:, None]).astype(np.float32),
        "w_words": wp[0],
        "w_scales": wp[1],
        "rw": (np.random.uniform(0.5, 2.0, (1, J))).astype(np.float32),
        "offs": striped(idx),
        "offs2": striped(idx2),
        "offs3": striped(idx3),
    }


def reference(xf, fk, w_words, w_scales, rw, offs, offs2, offs3):
    idx = unstriped(offs)
    idx2 = unstriped(offs2)
    idx3 = unstriped(offs3)
    wu = unpack_weight(w_words, w_scales, "e2m1")
    u = (np.maximum(f64(xf)[:, idx], np.maximum(f64(xf)[:, idx2], f64(xf)[:, idx3])) - 0.5 * f64(xf)[:, idx]) * f64(fk)
    uq = mxq(u, 0, "e4m3")
    p = wu.T @ uq
    y = p * f64(rw)
    return y

@@ -1,0 +1,186 @@
+from contextlib import ExitStack
+
+import concourse.mybir as mybir
+from concourse.masks import make_identity
+
+K, T, J, N = 1024, 1024, 512, 512
+FLOPS = 2 * K * J * N
+
+F32 = mybir.dt.float32
+BF16 = mybir.dt.bfloat16
+I32 = mybir.dt.int32
+U32 = mybir.dt.uint32
+U16 = mybir.dt.uint16
+U8 = mybir.dt.uint8
+FP8X4 = mybir.dt.float8_e4m3fn_x4
+FP4X4 = mybir.dt.float4_e2m1fn_x4
+ALU = mybir.AluOpType
+COPY = mybir.ActivationFunctionType.Copy
+
+P = 128
+PACK = 4
+PASSES = K // (P * PACK)
+CHUNK = 128
+UNITS = [(0, 0, 512), (1, 0, 256), (1, 256, 128), (1, 384, 128)]
+
+
+def tile_list_largest_of_three_lists_kernel(tc, xf, fk, w_words, w_scales, rw, offs, offs2, offs3, out):
+    nc = tc.nc
+    with ExitStack() as ctx:
+        keep = ctx.enter_context(tc.tile_pool(name="keep", bufs=1))
+        psum = ctx.enter_context(tc.psum_pool(name="psum", bufs=1))
+
+        lists = [keep.tile([P, J // 16], U16, name=f"list{i}") for i in range(3)]
+        planes = [[keep.tile([P, T], F32, name=f"x{a}{t}") for t in range(PACK)] for a in range(PASSES)]
+        rows = xf.rearrange("(a p t) c -> a t p c", a=PASSES, t=PACK)
+        factor = keep.tile([P, PASSES, PACK], F32)
+        half = keep.tile([P, PASSES, PACK], F32)
+        w_codes = [keep.tile([P, 2 * N], U8, name=f"wc{a}", align_bytes=64) for a in range(PASSES)]
+        w_plane = keep.tile([P, PASSES, N], U8, align_bytes=64)
+        weight = keep.tile([P, J], F32)
+        ident = keep.tile([P, P], F32)
+
+        nc.vector.memset(w_plane[:].rearrange("p a n -> p (a n)").bitcast(I32), 0)
+        make_identity(nc, ident[:])
+
+        nc.sync.dma_start(lists[0][:], offs)
+        nc.sync.dma_start(planes[0][0][:], rows[0, 0])
+        nc.sync.dma_start(lists[1][:], offs2)
+        nc.sync.dma_start(lists[2][:], offs3)
+        nc.sync.dma_start(planes[0][1][:], rows[0, 1])
+        nc.sync.dma_start(factor[:], fk.rearrange("(a p t) o -> p a (t o)", a=PASSES, t=PACK))
+        for a in range(PASSES):
+            for t in range(PACK):
+                if (a, t) > (0, 1):
+                    nc.sync.dma_start(planes[a][t][:], rows[a, t])
+        for a in range(PASSES):
+            nc.sync.dma_start(w_codes[a][:].bitcast(I32), w_words[a].bitcast(I32))
+        for q in range(4):
+            nc.sync.dma_start(
+                w_plane[32 * q : 32 * q + 4, :, :].bitcast(I32),
+                w_scales[:, 4 * q : 4 * q + 4, :].rearrange("a r n -> r a n").bitcast(I32),
+            )
+        nc.sync.dma_start(weight[:], rw[0].partition_broadcast(P))
+        nc.vector.tensor_scalar(half[:], factor[:], 0.5, None, ALU.mult)
+
+        steps = [(u, t) for u in range(len(UNITS)) for t in range(PACK)]
+        first, second, third, top = {}, {}, {}, {}
+        sums = {}
+        grouped = [keep.tile([P, unit[2], PACK], BF16, name=f"grouped{u}", align_bytes=64) for u, unit in enumerate(UNITS)]
+        u_codes = [keep.tile([P, J], U32, name=f"uc{a}", align_bytes=64) for a in range(PASSES)]
+        u_plane = [keep.tile([P, J], U8, name=f"us{a}", align_bytes=64) for a in range(PASSES)]
+
+        def picked(s, i):
+            u, t = steps[s]
+            a, j0, width = UNITS[u]
+            return planes[a][t][:].indirect(lists[i][:, j0 // 16 : (j0 + width) // 16])
+
+        def gather_first(s):
+            width = UNITS[steps[s][0]][2]
+            first[s] = keep.tile([P, width], F32, name=f"first{s}")
+            nc.vector.tensor_copy(first[s][:], picked(s, 0))
+
+        def gather_others(s):
+            width = UNITS[steps[s][0]][2]
+            second[s] = keep.tile([P, width], F32, name=f"second{s}")
+            third[s] = keep.tile([P, width], F32, name=f"third{s}")
+            nc.vector.tensor_tensor(second[s][:], picked(s, 1), first[s][:], ALU.subtract)
+            nc.vector.tensor_tensor(third[s][:], picked(s, 2), first[s][:], ALU.subtract)
+
+        def largest(s):
+            width = UNITS[steps[s][0]][2]
+            top[s] = keep.tile([P, width], F32, name=f"top{s}")
+            nc.vector.scalar_tensor_tensor(top[s][:], second[s][:], 0.0, third[s][:], ALU.max, ALU.max)
+
+        def scale_and_add(s):
+            u, t = steps[s]
+            a, j0, width = UNITS[u]
+            base = keep.tile([P, width], F32, name=f"base{s}")
+            gain = keep.tile([P, width], F32, name=f"gain{s}")
+            nc.scalar.activation(base[:], first[s][:], COPY, scale=half[:, a, t : t + 1])
+            nc.scalar.activation(gain[:], top[s][:], COPY, scale=factor[:, a, t : t + 1])
+            for c in range(j0 // CHUNK, (j0 + width) // CHUNK):
+                if t == 0:
+                    sums[a, c] = psum.tile([P, PACK, P], F32, name=f"sum{a}{c}", tag=f"bank{c}")
+                cols = slice(c * CHUNK - j0, (c + 1) * CHUNK - j0)
+                nc.tensor.matmul(sums[a, c][:, t, :], base[:, cols], ident[:], start=True, stop=False, is_transpose=True)
+                nc.tensor.matmul(sums[a, c][:, t, :], gain[:, cols], ident[:], start=False, stop=True, is_transpose=True)
+
+        def turn_back(u):
+            a, j0, width = UNITS[u]
+            for g0 in range(j0, j0 + width, 2 * CHUNK):
+                span = min(2 * CHUNK, j0 + width - g0)
+                back = psum.tile([P, 2, span], F32, name=f"back{a}{g0}", tag="bank4")
+                for c in range(g0 // CHUNK, (g0 + span) // CHUNK):
+                    rounded = keep.tile([P, 2, P, 2], BF16, name=f"rounded{a}{c}")
+                    nc.scalar.copy(rounded[:], sums[a, c][:].rearrange("j (h e) p -> j h p e", e=2))
+                    words = rounded[:].rearrange("j h p e -> j (h p e)").bitcast(F32)
+                    for h in range(2):
+                        nc.tensor.transpose(
+                            back[:, h, c * CHUNK - g0 : (c + 1) * CHUNK - g0], words[:, h * P : (h + 1) * P], ident[:]
+                        )
+                pairs = grouped[u][:, g0 - j0 : g0 - j0 + span, :].bitcast(F32)
+                nc.scalar.copy(pairs, back[:].rearrange("p h j -> p j h"))
+
+        def quantize(u):
+            a, j0, width = UNITS[u]
+            cols = slice(j0, j0 + width)
+            nc.vector.quantize_mx(
+                out=u_codes[a][:, cols].bitcast(FP8X4),
+                scales=u_plane[a][:, cols],
+                in_=grouped[u][:].rearrange("p j t -> p (j t)"),
+            )
+
+        def product(dst, nt, a, c):
+            cols = slice(c * CHUNK, (c + 1) * CHUNK)
+            nc.tensor.matmul_mx(
+                out=dst,
+                lhsT=w_codes[a][:, 2 * P * nt : 2 * P * (nt + 1)].bitcast(FP4X4),
+                lhsT_scale=w_plane[:, a, P * nt : P * (nt + 1)],
+                rhs=u_codes[a][:, cols].bitcast(FP8X4),
+                rhs_scale=u_plane[a][:, cols],
+                start=(a == 0),
+                stop=(a == PASSES - 1),
+            )
+
+        gather_first(0)
+        for s in range(len(steps)):
+            gather_others(s)
+            if s + 1 < len(steps):
+                gather_first(s + 1)
+            largest(s)
+            scale_and_add(s)
+            u, t = steps[s]
+            if t == PACK - 1:
+                turn_back(u)
+            if t == 1 and u > 0:
+                quantize(u - 1)
+
+        out_tiles = out.rearrange("(nt p) j -> p nt j", p=P)
+        last = J // CHUNK - 1
+        acc = {}
+        for c in range(last):
+            acc[c] = psum.tile([P, N // P, CHUNK], F32, name=f"acc{c}", tag=f"bank{5 + c}")
+            for nt in range(N // P):
+                for a in range(PASSES):
+                    product(acc[c][:, nt, :], nt, a, c)
+        ends = [psum.tile([P, CHUNK], F32, name=f"end{nt}", tag=f"bank{nt}") for nt in range(N // P)]
+        for nt in range(N // P):
+            product(ends[nt][:], nt, 0, last)
+        for c in range(last):
+            cols = slice(c * CHUNK, (c + 1) * CHUNK)
+            result = keep.tile([P, N // P, CHUNK], F32, name=f"result{c}")
+            nc.vector.tensor_tensor(
+                result[:], acc[c][:], weight[:, cols].unsqueeze(1).to_broadcast([P, N // P, CHUNK]), ALU.mult
+            )
+            nc.sync.dma_start(out_tiles[:, :, cols], result[:])
+        quantize(len(UNITS) - 1)
+        cols = slice(last * CHUNK, J)
+        for nt in range(N // P):
+            product(ends[nt][:], nt, 1, last)
+        for pair in range(2):
+            result = keep.tile([P, 2, CHUNK], F32, name=f"end_result{pair}")
+            for i in range(2):
+                nc.vector.tensor_tensor(result[:, i, :], ends[2 * pair + i][:], weight[:, cols], ALU.mult)
+            queue = nc.sync if pair == 0 else nc.scalar
+            queue.dma_start(out_tiles[:, 2 * pair : 2 * pair + 2, cols], result[:])

@@ -22,6 +22,8 @@ PACK = 4
 PASSES = K // (P * PACK)
 CHUNK = 128
 UNITS = [(0, 0, 512), (1, 0, 256), (1, 256, 128), (1, 384, 128)]
+REUSE = {8: 0, 12: 1, 14: 2}
+FINISH = {11: 0, 12: 1, 13: 2}
 
 
 def tile_list_largest_of_three_lists_kernel(tc, xf, fk, w_words, w_scales, rw, offs, offs2, offs3, out):
@@ -66,6 +68,7 @@ def tile_list_largest_of_three_lists_kernel(tc, xf, fk, w_words, w_scales, rw, o
         steps = [(u, t) for u in range(len(UNITS)) for t in range(PACK)]
         first, second, third, top = {}, {}, {}, {}
         sums = {}
+        early = keep.tile([P, PACK - 1, CHUNK], F32)
         grouped = [keep.tile([P, unit[2], PACK], BF16, name=f"grouped{u}", align_bytes=64) for u, unit in enumerate(UNITS)]
         u_codes = [keep.tile([P, J], U32, name=f"uc{a}", align_bytes=64) for a in range(PASSES)]
         u_plane = [keep.tile([P, J], U8, name=f"us{a}", align_bytes=64) for a in range(PASSES)]
@@ -77,15 +80,22 @@ def tile_list_largest_of_three_lists_kernel(tc, xf, fk, w_words, w_scales, rw, o
 
         def gather_first(s):
             width = UNITS[steps[s][0]][2]
-            first[s] = keep.tile([P, width], F32, name=f"first{s}")
-            nc.vector.tensor_copy(first[s][:], picked(s, 0))
+            if s in REUSE:
+                until = min([r for r in REUSE if r > s] + [len(steps)])
+                widths = [UNITS[steps[n][0]][2] for n in range(s, until)]
+                shared = keep.tile([P, sum(widths)], F32, name=f"firsts{s}", tag=f"grouped{REUSE[s]}", align_bytes=64)
+                for i, part in enumerate(widths):
+                    first[s + i] = shared[:, sum(widths[:i]) : sum(widths[: i + 1])]
+            if s not in first:
+                first[s] = keep.tile([P, width], F32, name=f"first{s}")[:]
+            nc.vector.tensor_copy(first[s], picked(s, 0))
 
         def gather_others(s):
             width = UNITS[steps[s][0]][2]
             second[s] = keep.tile([P, width], F32, name=f"second{s}")
             third[s] = keep.tile([P, width], F32, name=f"third{s}")
-            nc.vector.tensor_tensor(second[s][:], picked(s, 1), first[s][:], ALU.subtract)
-            nc.vector.tensor_tensor(third[s][:], picked(s, 2), first[s][:], ALU.subtract)
+            nc.vector.tensor_tensor(second[s][:], picked(s, 1), first[s], ALU.subtract)
+            nc.vector.tensor_tensor(third[s][:], picked(s, 2), first[s], ALU.subtract)
 
         def largest(s):
             width = UNITS[steps[s][0]][2]
@@ -96,12 +106,22 @@ def tile_list_largest_of_three_lists_kernel(tc, xf, fk, w_words, w_scales, rw, o
             u, t = steps[s]
             a, j0, width = UNITS[u]
             base = keep.tile([P, width], F32, name=f"base{s}")
-            gain = keep.tile([P, width], F32, name=f"gain{s}")
-            nc.scalar.activation(base[:], first[s][:], COPY, scale=half[:, a, t : t + 1])
+            nc.scalar.activation(base[:], first[s], COPY, scale=half[:, a, t : t + 1])
+            if u == len(UNITS) - 1:
+                whole = grouped[u][:, :, t] if t == PACK - 1 else early[:, t, :]
+                nc.vector.scalar_tensor_tensor(whole, top[s][:], factor[:, a, t : t + 1], base[:], ALU.mult, ALU.add)
+                if t == PACK - 2:
+                    nc.vector.tensor_copy(grouped[u][:, :, 0 : PACK - 1], early[:].rearrange("p t j -> p j t"))
+                return
+            tag = f"gain{s}"
+            if s + 1 in REUSE:
+                done_pass, done_start, done_width = UNITS[REUSE[s + 1]]
+                tag = f"rounded{done_pass}{(done_start + done_width) // CHUNK - 1}"
+            gain = keep.tile([P, width], F32, name=f"gain{s}", tag=tag)
             nc.scalar.activation(gain[:], top[s][:], COPY, scale=factor[:, a, t : t + 1])
             for c in range(j0 // CHUNK, (j0 + width) // CHUNK):
                 if t == 0:
-                    sums[a, c] = psum.tile([P, PACK, P], F32, name=f"sum{a}{c}", tag=f"bank{c}")
+                    sums[a, c] = psum.tile([P, PACK, P], F32, name=f"sum{a}{c}", tag="sum", bufs=4)
                 cols = slice(c * CHUNK - j0, (c + 1) * CHUNK - j0)
                 nc.tensor.matmul(sums[a, c][:, t, :], base[:, cols], ident[:], start=True, stop=False, is_transpose=True)
                 nc.tensor.matmul(sums[a, c][:, t, :], gain[:, cols], ident[:], start=False, stop=True, is_transpose=True)
@@ -110,7 +130,7 @@ def tile_list_largest_of_three_lists_kernel(tc, xf, fk, w_words, w_scales, rw, o
             a, j0, width = UNITS[u]
             for g0 in range(j0, j0 + width, 2 * CHUNK):
                 span = min(2 * CHUNK, j0 + width - g0)
-                back = psum.tile([P, 2, span], F32, name=f"back{a}{g0}", tag="bank4")
+                back = psum.tile([P, 2, span], F32, name=f"back{a}{g0}", tag="back")
                 for c in range(g0 // CHUNK, (g0 + span) // CHUNK):
                     rounded = keep.tile([P, 2, P, 2], BF16, name=f"rounded{a}{c}")
                     nc.scalar.copy(rounded[:], sums[a, c][:].rearrange("j (h e) p -> j h p e", e=2))
@@ -131,7 +151,7 @@ def tile_list_largest_of_three_lists_kernel(tc, xf, fk, w_words, w_scales, rw, o
                 in_=grouped[u][:].rearrange("p j t -> p (j t)"),
             )
 
-        def product(dst, nt, a, c):
+        def product(dst, nt, a, c, place):
             cols = slice(c * CHUNK, (c + 1) * CHUNK)
             nc.tensor.matmul_mx(
                 out=dst,
@@ -139,48 +159,78 @@ def tile_list_largest_of_three_lists_kernel(tc, xf, fk, w_words, w_scales, rw, o
                 lhsT_scale=w_plane[:, a, P * nt : P * (nt + 1)],
                 rhs=u_codes[a][:, cols].bitcast(FP8X4),
                 rhs_scale=u_plane[a][:, cols],
-                start=(a == 0),
-                stop=(a == PASSES - 1),
+                start=(place == 0),
+                stop=(place == PASSES - 1),
             )
+
+        out_tiles = out.rearrange("(nt p) j -> p nt j", p=P)
+        last = J // CHUNK - 1
+        turned_weight = psum.tile([P, last, P], F32, name="turned_weight", tag="out")
+        for c in range(last):
+            nc.tensor.transpose(turned_weight[:, c, :], weight[:, c * CHUNK : (c + 1) * CHUNK], ident[:])
+        slot_weight = keep.tile([P, last], F32)
+        nc.scalar.copy(slot_weight[:], turned_weight[:, :, 0])
+
+        acc = {}
+
+        def multiply(u):
+            a, j0, width = UNITS[u]
+            for c in range(j0 // CHUNK, (j0 + width) // CHUNK):
+                cols = slice(c * CHUNK, (c + 1) * CHUNK)
+                acc[c] = psum.tile([P, N], F32, name=f"acc{c}", tag="acc", bufs=2)
+                for i in range(PASSES):
+                    k = i
+                    nc.tensor.matmul_mx(
+                        out=acc[c][:],
+                        lhsT=u_codes[k][:, cols].bitcast(FP8X4),
+                        lhsT_scale=u_plane[k][:, cols],
+                        rhs=w_codes[k][:].bitcast(FP4X4),
+                        rhs_scale=w_plane[:, k, :],
+                        start=(i == 0),
+                        stop=(i == PASSES - 1),
+                    )
+
+        def finish(c):
+            cols = slice(c * CHUNK, (c + 1) * CHUNK)
+            scaled = keep.tile([P, N], F32, name=f"scaled{c}")
+            nc.scalar.activation(scaled[:], acc[c][:], COPY, scale=slot_weight[:, c : c + 1])
+            upright = psum.tile([P, N // P, CHUNK], F32, name=f"upright{c}", tag="out")
+            for nt in range(N // P):
+                nc.tensor.transpose(upright[:, nt, :], scaled[:, nt * P : (nt + 1) * P], ident[:])
+            result = keep.tile([P, N // P, CHUNK], F32, name=f"result{c}")
+            nc.scalar.copy(result[:], upright[:])
+            nc.sync.dma_start(out_tiles[:, :, cols], result[:])
 
         gather_first(0)
         for s in range(len(steps)):
             gather_others(s)
+            if s + 1 in REUSE:
+                quantize(REUSE[s + 1])
             if s + 1 < len(steps):
                 gather_first(s + 1)
             largest(s)
             scale_and_add(s)
             u, t = steps[s]
-            if t == PACK - 1:
+            if t == PACK - 1 and u < len(UNITS) - 1:
                 turn_back(u)
-            if t == 1 and u > 0:
-                quantize(u - 1)
+            if s + 1 in REUSE and UNITS[REUSE[s + 1]][0] == PASSES - 1:
+                multiply(REUSE[s + 1])
+            if s in FINISH:
+                finish(FINISH[s])
 
-        out_tiles = out.rearrange("(nt p) j -> p nt j", p=P)
-        last = J // CHUNK - 1
-        acc = {}
-        for c in range(last):
-            acc[c] = psum.tile([P, N // P, CHUNK], F32, name=f"acc{c}", tag=f"bank{5 + c}")
-            for nt in range(N // P):
-                for a in range(PASSES):
-                    product(acc[c][:, nt, :], nt, a, c)
-        ends = [psum.tile([P, CHUNK], F32, name=f"end{nt}", tag=f"bank{nt}") for nt in range(N // P)]
+        ends = [psum.tile([P, CHUNK], F32, name=f"end{nt}", tag="sum", bufs=4) for nt in range(N // P)]
         for nt in range(N // P):
-            product(ends[nt][:], nt, 0, last)
-        for c in range(last):
-            cols = slice(c * CHUNK, (c + 1) * CHUNK)
-            result = keep.tile([P, N // P, CHUNK], F32, name=f"result{c}")
-            nc.vector.tensor_tensor(
-                result[:], acc[c][:], weight[:, cols].unsqueeze(1).to_broadcast([P, N // P, CHUNK]), ALU.mult
-            )
-            nc.sync.dma_start(out_tiles[:, :, cols], result[:])
+            product(ends[nt][:], nt, 0, last, 0)
         quantize(len(UNITS) - 1)
         cols = slice(last * CHUNK, J)
         for nt in range(N // P):
-            product(ends[nt][:], nt, 1, last)
+            product(ends[nt][:], nt, 1, last, 1)
         for pair in range(2):
             result = keep.tile([P, 2, CHUNK], F32, name=f"end_result{pair}")
             for i in range(2):
                 nc.vector.tensor_tensor(result[:, i, :], ends[2 * pair + i][:], weight[:, cols], ALU.mult)
             queue = nc.sync if pair == 0 else nc.scalar
             queue.dma_start(out_tiles[:, 2 * pair : 2 * pair + 2, cols], result[:])
+        for c in range(last):
+            if c not in FINISH.values():
+                finish(c)

@@ -22,8 +22,9 @@ PACK = 4
 PASSES = K // (P * PACK)
 CHUNK = 128
 UNITS = [(0, 0, 512), (1, 0, 256), (1, 256, 128), (1, 384, 128)]
-REUSE = {8: 0, 12: 1, 14: 2}
-FINISH = {11: 0, 12: 1, 13: 2}
+REUSE = {8: 0, 12: 1, 15: 2}
+FINISH = {11: 0, 12: 1, 14: 2}
+RUN_START = {0: 0, 1: 1, 2: 2, 3: 3}
 
 
 def tile_list_largest_of_three_lists_kernel(tc, xf, fk, w_words, w_scales, rw, offs, offs2, offs3, out):
@@ -45,8 +46,8 @@ def tile_list_largest_of_three_lists_kernel(tc, xf, fk, w_words, w_scales, rw, o
         nc.vector.memset(w_plane[:].rearrange("p a n -> p (a n)").bitcast(I32), 0)
         make_identity(nc, ident[:])
 
-        nc.sync.dma_start(lists[0][:], offs)
         nc.sync.dma_start(planes[0][0][:], rows[0, 0])
+        nc.sync.dma_start(lists[0][:], offs)
         nc.sync.dma_start(lists[1][:], offs2)
         nc.sync.dma_start(lists[2][:], offs3)
         nc.sync.dma_start(planes[0][1][:], rows[0, 1])
@@ -63,7 +64,7 @@ def tile_list_largest_of_three_lists_kernel(tc, xf, fk, w_words, w_scales, rw, o
                 w_scales[:, 4 * q : 4 * q + 4, :].rearrange("a r n -> r a n").bitcast(I32),
             )
         nc.sync.dma_start(weight[:], rw[0].partition_broadcast(P))
-        nc.vector.tensor_scalar(half[:], factor[:], 0.5, None, ALU.mult)
+        nc.scalar.activation(half[:], factor[:], COPY, scale=0.5)
 
         steps = [(u, t) for u in range(len(UNITS)) for t in range(PACK)]
         first, second, third, top = {}, {}, {}, {}
@@ -91,16 +92,18 @@ def tile_list_largest_of_three_lists_kernel(tc, xf, fk, w_words, w_scales, rw, o
             nc.vector.tensor_copy(first[s], picked(s, 0))
 
         def gather_others(s):
-            width = UNITS[steps[s][0]][2]
-            second[s] = keep.tile([P, width], F32, name=f"second{s}")
-            third[s] = keep.tile([P, width], F32, name=f"third{s}")
-            nc.vector.tensor_tensor(second[s][:], picked(s, 1), first[s], ALU.subtract)
-            nc.vector.tensor_tensor(third[s][:], picked(s, 2), first[s], ALU.subtract)
+            u, t = steps[s]
+            if t == 0:
+                second[u] = keep.tile([P, PACK, UNITS[u][2]], F32, name=f"second{u}")
+                third[u] = keep.tile([P, PACK, UNITS[u][2]], F32, name=f"third{u}")
+                top[u] = keep.tile([P, PACK, UNITS[u][2]], F32, name=f"top{u}")
+            nc.vector.tensor_tensor(second[u][:, t, :], picked(s, 1), first[s], ALU.subtract)
+            nc.vector.tensor_tensor(third[u][:, t, :], picked(s, 2), first[s], ALU.subtract)
 
-        def largest(s):
-            width = UNITS[steps[s][0]][2]
-            top[s] = keep.tile([P, width], F32, name=f"top{s}")
-            nc.vector.scalar_tensor_tensor(top[s][:], second[s][:], 0.0, third[s][:], ALU.max, ALU.max)
+        def largest(u, run):
+            nc.vector.scalar_tensor_tensor(
+                top[u][:, run, :], second[u][:, run, :], 0.0, third[u][:, run, :], ALU.max, ALU.max
+            )
 
         def scale_and_add(s):
             u, t = steps[s]
@@ -109,7 +112,7 @@ def tile_list_largest_of_three_lists_kernel(tc, xf, fk, w_words, w_scales, rw, o
             nc.scalar.activation(base[:], first[s], COPY, scale=half[:, a, t : t + 1])
             if u == len(UNITS) - 1:
                 whole = grouped[u][:, :, t] if t == PACK - 1 else early[:, t, :]
-                nc.vector.scalar_tensor_tensor(whole, top[s][:], factor[:, a, t : t + 1], base[:], ALU.mult, ALU.add)
+                nc.vector.scalar_tensor_tensor(whole, top[u][:, t, :], factor[:, a, t : t + 1], base[:], ALU.mult, ALU.add)
                 if t == PACK - 2:
                     nc.vector.tensor_copy(grouped[u][:, :, 0 : PACK - 1], early[:].rearrange("p t j -> p j t"))
                 return
@@ -118,10 +121,10 @@ def tile_list_largest_of_three_lists_kernel(tc, xf, fk, w_words, w_scales, rw, o
                 done_pass, done_start, done_width = UNITS[REUSE[s + 1]]
                 tag = f"rounded{done_pass}{(done_start + done_width) // CHUNK - 1}"
             gain = keep.tile([P, width], F32, name=f"gain{s}", tag=tag)
-            nc.scalar.activation(gain[:], top[s][:], COPY, scale=factor[:, a, t : t + 1])
+            nc.scalar.activation(gain[:], top[u][:, t, :], COPY, scale=factor[:, a, t : t + 1])
             for c in range(j0 // CHUNK, (j0 + width) // CHUNK):
                 if t == 0:
-                    sums[a, c] = psum.tile([P, PACK, P], F32, name=f"sum{a}{c}", tag="sum", bufs=4)
+                    sums[a, c] = psum.tile([P, PACK, P], F32, name=f"sum{a}{c}", tag=f"sum{c}")
                 cols = slice(c * CHUNK - j0, (c + 1) * CHUNK - j0)
                 nc.tensor.matmul(sums[a, c][:, t, :], base[:, cols], ident[:], start=True, stop=False, is_transpose=True)
                 nc.tensor.matmul(sums[a, c][:, t, :], gain[:, cols], ident[:], start=False, stop=True, is_transpose=True)
@@ -151,7 +154,7 @@ def tile_list_largest_of_three_lists_kernel(tc, xf, fk, w_words, w_scales, rw, o
                 in_=grouped[u][:].rearrange("p j t -> p (j t)"),
             )
 
-        def product(dst, nt, a, c, place):
+        def product(dst, nt, a, c, start, stop):
             cols = slice(c * CHUNK, (c + 1) * CHUNK)
             nc.tensor.matmul_mx(
                 out=dst,
@@ -159,17 +162,19 @@ def tile_list_largest_of_three_lists_kernel(tc, xf, fk, w_words, w_scales, rw, o
                 lhsT_scale=w_plane[:, a, P * nt : P * (nt + 1)],
                 rhs=u_codes[a][:, cols].bitcast(FP8X4),
                 rhs_scale=u_plane[a][:, cols],
-                start=(place == 0),
-                stop=(place == PASSES - 1),
+                start=start,
+                stop=stop,
             )
 
         out_tiles = out.rearrange("(nt p) j -> p nt j", p=P)
         last = J // CHUNK - 1
-        turned_weight = psum.tile([P, last, P], F32, name="turned_weight", tag="out")
-        for c in range(last):
-            nc.tensor.transpose(turned_weight[:, c, :], weight[:, c * CHUNK : (c + 1) * CHUNK], ident[:])
         slot_weight = keep.tile([P, last], F32)
-        nc.scalar.copy(slot_weight[:], turned_weight[:, :, 0])
+
+        def turn_weights():
+            turned_weight = psum.tile([P, last, P], F32, name="turned_weight", tag="out")
+            for c in range(last):
+                nc.tensor.transpose(turned_weight[:, c, :], weight[:, c * CHUNK : (c + 1) * CHUNK], ident[:])
+            nc.scalar.copy(slot_weight[:], turned_weight[:, :, 0])
 
         acc = {}
 
@@ -208,9 +213,15 @@ def tile_list_largest_of_three_lists_kernel(tc, xf, fk, w_words, w_scales, rw, o
                 quantize(REUSE[s + 1])
             if s + 1 < len(steps):
                 gather_first(s + 1)
-            largest(s)
-            scale_and_add(s)
             u, t = steps[s]
+            if t in RUN_START:
+                largest(u, slice(RUN_START[t], t + 1))
+                for n in range(s - t + RUN_START[t], s + 1):
+                    scale_and_add(n)
+            if s == 0:
+                turn_weights()
+            if s == 5 and 0 not in REUSE.values():
+                quantize(0)
             if t == PACK - 1 and u < len(UNITS) - 1:
                 turn_back(u)
             if s + 1 in REUSE and UNITS[REUSE[s + 1]][0] == PASSES - 1:
@@ -218,19 +229,17 @@ def tile_list_largest_of_three_lists_kernel(tc, xf, fk, w_words, w_scales, rw, o
             if s in FINISH:
                 finish(FINISH[s])
 
-        ends = [psum.tile([P, CHUNK], F32, name=f"end{nt}", tag="sum", bufs=4) for nt in range(N // P)]
+        ends = [psum.tile([P, 2, CHUNK], F32, name=f"end{pair}", tag=tag) for pair, tag in enumerate(("sum0", "sum1"))]
         for nt in range(N // P):
-            product(ends[nt][:], nt, 0, last, 0)
+            product(ends[nt // 2][:, nt % 2, :], nt, 0, last, nt % 2 == 0, False)
         quantize(len(UNITS) - 1)
         cols = slice(last * CHUNK, J)
         for nt in range(N // P):
-            product(ends[nt][:], nt, 1, last, 1)
+            product(ends[nt // 2][:, nt % 2, :], nt, 1, last, False, nt % 2 == 1)
         for pair in range(2):
             result = keep.tile([P, 2, CHUNK], F32, name=f"end_result{pair}")
-            for i in range(2):
-                nc.vector.tensor_tensor(result[:, i, :], ends[2 * pair + i][:], weight[:, cols], ALU.mult)
+            nc.vector.tensor_tensor(
+                result[:], ends[pair][:], weight[:, cols].unsqueeze(1).to_broadcast([P, 2, CHUNK]), ALU.mult
+            )
             queue = nc.sync if pair == 0 else nc.scalar
             queue.dma_start(out_tiles[:, 2 * pair : 2 * pair + 2, cols], result[:])
-        for c in range(last):
-            if c not in FINISH.values():
-                finish(c)

from contextlib import ExitStack

import concourse.mybir as mybir
from concourse.masks import make_identity

K, T, J, N = 1024, 1024, 512, 512
FLOPS = 2 * K * J * N

F32 = mybir.dt.float32
BF16 = mybir.dt.bfloat16
I32 = mybir.dt.int32
U32 = mybir.dt.uint32
U16 = mybir.dt.uint16
U8 = mybir.dt.uint8
FP8X4 = mybir.dt.float8_e4m3fn_x4
FP4X4 = mybir.dt.float4_e2m1fn_x4
ALU = mybir.AluOpType
COPY = mybir.ActivationFunctionType.Copy

P = 128
PACK = 4
PASSES = K // (P * PACK)
CHUNK = 128
UNITS = [(0, 0, 512), (1, 0, 256), (1, 256, 128), (1, 384, 128)]
REUSE = {8: 0, 12: 1, 15: 2}
FINISH = {11: 0, 12: 1, 14: 2}
RUN_START = {0: 0, 1: 1, 2: 2, 3: 3}


def tile_list_largest_of_three_lists_kernel(tc, xf, fk, w_words, w_scales, rw, offs, offs2, offs3, out):
    nc = tc.nc
    with ExitStack() as ctx:
        keep = ctx.enter_context(tc.tile_pool(name="keep", bufs=1))
        psum = ctx.enter_context(tc.psum_pool(name="psum", bufs=1))

        lists = [keep.tile([P, J // 16], U16, name=f"list{i}") for i in range(3)]
        planes = [[keep.tile([P, T], F32, name=f"x{a}{t}") for t in range(PACK)] for a in range(PASSES)]
        rows = xf.rearrange("(a p t) c -> a t p c", a=PASSES, t=PACK)
        factor = keep.tile([P, PASSES, PACK], F32)
        half = keep.tile([P, PASSES, PACK], F32)
        w_codes = [keep.tile([P, 2 * N], U8, name=f"wc{a}", align_bytes=64) for a in range(PASSES)]
        w_plane = keep.tile([P, PASSES, N], U8, align_bytes=64)
        weight = keep.tile([P, J], F32)
        ident = keep.tile([P, P], F32)

        nc.vector.memset(w_plane[:].rearrange("p a n -> p (a n)").bitcast(I32), 0)
        make_identity(nc, ident[:])

        nc.sync.dma_start(planes[0][0][:], rows[0, 0])
        nc.sync.dma_start(lists[0][:], offs)
        nc.sync.dma_start(lists[1][:], offs2)
        nc.sync.dma_start(lists[2][:], offs3)
        nc.sync.dma_start(planes[0][1][:], rows[0, 1])
        nc.sync.dma_start(factor[:], fk.rearrange("(a p t) o -> p a (t o)", a=PASSES, t=PACK))
        for a in range(PASSES):
            for t in range(PACK):
                if (a, t) > (0, 1):
                    nc.sync.dma_start(planes[a][t][:], rows[a, t])
        for a in range(PASSES):
            nc.sync.dma_start(w_codes[a][:].bitcast(I32), w_words[a].bitcast(I32))
        for q in range(4):
            nc.sync.dma_start(
                w_plane[32 * q : 32 * q + 4, :, :].bitcast(I32),
                w_scales[:, 4 * q : 4 * q + 4, :].rearrange("a r n -> r a n").bitcast(I32),
            )
        nc.sync.dma_start(weight[:], rw[0].partition_broadcast(P))
        nc.scalar.activation(half[:], factor[:], COPY, scale=0.5)

        steps = [(u, t) for u in range(len(UNITS)) for t in range(PACK)]
        first, second, third, top = {}, {}, {}, {}
        sums = {}
        early = keep.tile([P, PACK - 1, CHUNK], F32)
        grouped = [keep.tile([P, unit[2], PACK], BF16, name=f"grouped{u}", align_bytes=64) for u, unit in enumerate(UNITS)]
        u_codes = [keep.tile([P, J], U32, name=f"uc{a}", align_bytes=64) for a in range(PASSES)]
        u_plane = [keep.tile([P, J], U8, name=f"us{a}", align_bytes=64) for a in range(PASSES)]

        def picked(s, i):
            u, t = steps[s]
            a, j0, width = UNITS[u]
            return planes[a][t][:].indirect(lists[i][:, j0 // 16 : (j0 + width) // 16])

        def gather_first(s):
            width = UNITS[steps[s][0]][2]
            if s in REUSE:
                until = min([r for r in REUSE if r > s] + [len(steps)])
                widths = [UNITS[steps[n][0]][2] for n in range(s, until)]
                shared = keep.tile([P, sum(widths)], F32, name=f"firsts{s}", tag=f"grouped{REUSE[s]}", align_bytes=64)
                for i, part in enumerate(widths):
                    first[s + i] = shared[:, sum(widths[:i]) : sum(widths[: i + 1])]
            if s not in first:
                first[s] = keep.tile([P, width], F32, name=f"first{s}")[:]
            nc.vector.tensor_copy(first[s], picked(s, 0))

        def gather_others(s):
            u, t = steps[s]
            if t == 0:
                second[u] = keep.tile([P, PACK, UNITS[u][2]], F32, name=f"second{u}")
                third[u] = keep.tile([P, PACK, UNITS[u][2]], F32, name=f"third{u}")
                top[u] = keep.tile([P, PACK, UNITS[u][2]], F32, name=f"top{u}")
            nc.vector.tensor_tensor(second[u][:, t, :], picked(s, 1), first[s], ALU.subtract)
            nc.vector.tensor_tensor(third[u][:, t, :], picked(s, 2), first[s], ALU.subtract)

        def largest(u, run):
            nc.vector.scalar_tensor_tensor(
                top[u][:, run, :], second[u][:, run, :], 0.0, third[u][:, run, :], ALU.max, ALU.max
            )

        def scale_and_add(s):
            u, t = steps[s]
            a, j0, width = UNITS[u]
            base = keep.tile([P, width], F32, name=f"base{s}")
            nc.scalar.activation(base[:], first[s], COPY, scale=half[:, a, t : t + 1])
            if u == len(UNITS) - 1:
                whole = grouped[u][:, :, t] if t == PACK - 1 else early[:, t, :]
                nc.vector.scalar_tensor_tensor(whole, top[u][:, t, :], factor[:, a, t : t + 1], base[:], ALU.mult, ALU.add)
                if t == PACK - 2:
                    nc.vector.tensor_copy(grouped[u][:, :, 0 : PACK - 1], early[:].rearrange("p t j -> p j t"))
                return
            tag = f"gain{s}"
            if s + 1 in REUSE:
                done_pass, done_start, done_width = UNITS[REUSE[s + 1]]
                tag = f"rounded{done_pass}{(done_start + done_width) // CHUNK - 1}"
            gain = keep.tile([P, width], F32, name=f"gain{s}", tag=tag)
            nc.scalar.activation(gain[:], top[u][:, t, :], COPY, scale=factor[:, a, t : t + 1])
            for c in range(j0 // CHUNK, (j0 + width) // CHUNK):
                if t == 0:
                    sums[a, c] = psum.tile([P, PACK, P], F32, name=f"sum{a}{c}", tag=f"sum{c}")
                cols = slice(c * CHUNK - j0, (c + 1) * CHUNK - j0)
                nc.tensor.matmul(sums[a, c][:, t, :], base[:, cols], ident[:], start=True, stop=False, is_transpose=True)
                nc.tensor.matmul(sums[a, c][:, t, :], gain[:, cols], ident[:], start=False, stop=True, is_transpose=True)

        def turn_back(u):
            a, j0, width = UNITS[u]
            for g0 in range(j0, j0 + width, 2 * CHUNK):
                span = min(2 * CHUNK, j0 + width - g0)
                back = psum.tile([P, 2, span], F32, name=f"back{a}{g0}", tag="back")
                for c in range(g0 // CHUNK, (g0 + span) // CHUNK):
                    rounded = keep.tile([P, 2, P, 2], BF16, name=f"rounded{a}{c}")
                    nc.scalar.copy(rounded[:], sums[a, c][:].rearrange("j (h e) p -> j h p e", e=2))
                    words = rounded[:].rearrange("j h p e -> j (h p e)").bitcast(F32)
                    for h in range(2):
                        nc.tensor.transpose(
                            back[:, h, c * CHUNK - g0 : (c + 1) * CHUNK - g0], words[:, h * P : (h + 1) * P], ident[:]
                        )
                pairs = grouped[u][:, g0 - j0 : g0 - j0 + span, :].bitcast(F32)
                nc.scalar.copy(pairs, back[:].rearrange("p h j -> p j h"))

        def quantize(u):
            a, j0, width = UNITS[u]
            cols = slice(j0, j0 + width)
            nc.vector.quantize_mx(
                out=u_codes[a][:, cols].bitcast(FP8X4),
                scales=u_plane[a][:, cols],
                in_=grouped[u][:].rearrange("p j t -> p (j t)"),
            )

        def product(dst, nt, a, c, start, stop):
            cols = slice(c * CHUNK, (c + 1) * CHUNK)
            nc.tensor.matmul_mx(
                out=dst,
                lhsT=w_codes[a][:, 2 * P * nt : 2 * P * (nt + 1)].bitcast(FP4X4),
                lhsT_scale=w_plane[:, a, P * nt : P * (nt + 1)],
                rhs=u_codes[a][:, cols].bitcast(FP8X4),
                rhs_scale=u_plane[a][:, cols],
                start=start,
                stop=stop,
            )

        out_tiles = out.rearrange("(nt p) j -> p nt j", p=P)
        last = J // CHUNK - 1
        slot_weight = keep.tile([P, last], F32)

        def turn_weights():
            turned_weight = psum.tile([P, last, P], F32, name="turned_weight", tag="out")
            for c in range(last):
                nc.tensor.transpose(turned_weight[:, c, :], weight[:, c * CHUNK : (c + 1) * CHUNK], ident[:])
            nc.scalar.copy(slot_weight[:], turned_weight[:, :, 0])

        acc = {}

        def multiply(u):
            a, j0, width = UNITS[u]
            for c in range(j0 // CHUNK, (j0 + width) // CHUNK):
                cols = slice(c * CHUNK, (c + 1) * CHUNK)
                acc[c] = psum.tile([P, N], F32, name=f"acc{c}", tag="acc", bufs=2)
                for i in range(PASSES):
                    k = i
                    nc.tensor.matmul_mx(
                        out=acc[c][:],
                        lhsT=u_codes[k][:, cols].bitcast(FP8X4),
                        lhsT_scale=u_plane[k][:, cols],
                        rhs=w_codes[k][:].bitcast(FP4X4),
                        rhs_scale=w_plane[:, k, :],
                        start=(i == 0),
                        stop=(i == PASSES - 1),
                    )

        def finish(c):
            cols = slice(c * CHUNK, (c + 1) * CHUNK)
            scaled = keep.tile([P, N], F32, name=f"scaled{c}")
            nc.scalar.activation(scaled[:], acc[c][:], COPY, scale=slot_weight[:, c : c + 1])
            upright = psum.tile([P, N // P, CHUNK], F32, name=f"upright{c}", tag="out")
            for nt in range(N // P):
                nc.tensor.transpose(upright[:, nt, :], scaled[:, nt * P : (nt + 1) * P], ident[:])
            result = keep.tile([P, N // P, CHUNK], F32, name=f"result{c}")
            nc.scalar.copy(result[:], upright[:])
            nc.sync.dma_start(out_tiles[:, :, cols], result[:])

        gather_first(0)
        for s in range(len(steps)):
            gather_others(s)
            if s + 1 in REUSE:
                quantize(REUSE[s + 1])
            if s + 1 < len(steps):
                gather_first(s + 1)
            u, t = steps[s]
            if t in RUN_START:
                largest(u, slice(RUN_START[t], t + 1))
                for n in range(s - t + RUN_START[t], s + 1):
                    scale_and_add(n)
            if s == 0:
                turn_weights()
            if s == 5 and 0 not in REUSE.values():
                quantize(0)
            if t == PACK - 1 and u < len(UNITS) - 1:
                turn_back(u)
            if s + 1 in REUSE and UNITS[REUSE[s + 1]][0] == PASSES - 1:
                multiply(REUSE[s + 1])
            if s in FINISH:
                finish(FINISH[s])

        ends = [psum.tile([P, 2, CHUNK], F32, name=f"end{pair}", tag=tag) for pair, tag in enumerate(("sum0", "sum1"))]
        for nt in range(N // P):
            product(ends[nt // 2][:, nt % 2, :], nt, 0, last, nt % 2 == 0, False)
        quantize(len(UNITS) - 1)
        cols = slice(last * CHUNK, J)
        for nt in range(N // P):
            product(ends[nt // 2][:, nt % 2, :], nt, 1, last, False, nt % 2 == 1)
        for pair in range(2):
            result = keep.tile([P, 2, CHUNK], F32, name=f"end_result{pair}")
            nc.vector.tensor_tensor(
                result[:], ends[pair][:], weight[:, cols].unsqueeze(1).to_broadcast([P, 2, CHUNK]), ALU.mult
            )
            queue = nc.sync if pair == 0 else nc.scalar
            queue.dma_start(out_tiles[:, 2 * pair : 2 * pair + 2, cols], result[:])
